import numpy as np
import ml_dtypes


def mxq(x, axis, fmt="e4m3"):
    dtype, down = {"e4m3": (ml_dtypes.float8_e4m3fn, 7), "e5m2": (ml_dtypes.float8_e5m2, 14)}[fmt]
    v = np.moveaxis(np.asarray(x, np.float32).astype(ml_dtypes.bfloat16).astype(np.float64), axis, -1)
    blocks = v.reshape(v.shape[:-1] + (-1, 32))
    amax = np.abs(blocks).max(-1, keepdims=True)
    byte = np.maximum(np.where(amax > 0, np.frexp(amax)[1] - 1 + 127, 0) - down, 1)
    scale = np.exp2(byte - 127.0)
    codes = (blocks / scale).astype(np.float32).astype(dtype).astype(np.float64)
    return np.moveaxis((codes * scale).reshape(v.shape), -1, axis)


WIDE = False


def mx_kscale(k):
    if not WIDE:
        return np.ones(k)
    levels = np.array([10, -10, 5, -5, 0])
    if k % 512:
        return np.exp2(np.random.permutation(np.resize(levels, k // 32))).repeat(32)
    a = np.empty((k // 512, 16))
    for p in range(k // 512):
        a[p, :8] = np.random.permutation(np.resize(levels, 8))
        for g in range(8):
            far = levels[np.abs(levels - a[p, g]) >= 10]
            a[p, g + 8] = far[np.random.randint(len(far))]
    return np.exp2(a.ravel()).repeat(32)


def f64(x):
    return np.asarray(x).astype(np.float64)


def striped8(idx):
    return np.asarray(idx).reshape(8, -1, 16).transpose(0, 2, 1).reshape(128, -1).astype(np.uint16)


def unstriped8(offs):
    return offs.reshape(8, 16, -1).transpose(0, 2, 1).reshape(8, -1).astype(np.int64)


def pick8(x, idx, run):
    r = np.arange(len(x))
    return x[r[:, None], idx[r % (8 * run) // run]]


E2M1 = np.array([0.0, 0.5, 1.0, 1.5, 2.0, 3.0, 4.0, 6.0, -0.0, -0.5, -1.0, -1.5, -2.0, -3.0, -4.0, -6.0])


def pack_weight(w, fmt):
    k, n = w.shape
    w = f64(np.asarray(w, np.float32).astype(ml_dtypes.bfloat16)).reshape(k // 32, 32, n)
    amax = np.abs(w).max(1)
    if fmt == "e4m3":
        byte = np.frexp(amax)[1] - 1 + 127 - 7
    else:
        mant, ex = np.frexp(amax / 6.0)
        byte = np.where(mant > 0.5, ex, ex - 1) + 127
    byte = np.clip(np.where(amax > 0, byte, 1), 1, 254)
    scaled = (w * np.exp2(127.0 - byte)[:, None, :]).reshape(k, n).astype(np.float32)
    by_word = np.ascontiguousarray(scaled.reshape(k // 512, 128, 4, n).transpose(0, 1, 3, 2))
    if fmt == "e4m3":
        words = by_word.astype(ml_dtypes.float8_e4m3fn).view(np.uint8)
    else:
        c = by_word.astype(ml_dtypes.float4_e2m1fn).view(np.uint8) & 0xF
        words = (c[..., 0::2] | (c[..., 1::2] << 4)).reshape(k // 512, 128, 2 * n)
    return np.ascontiguousarray(words), np.ascontiguousarray(byte.astype(np.uint8).reshape(k // 512, 16, n))


def unpack_weight(words, scales, fmt):
    g, _, n = scales.shape
    words = np.ascontiguousarray(words).reshape(g, 128, n, -1)
    if fmt == "e4m3":
        vals = words.view(ml_dtypes.float8_e4m3fn).astype(np.float64)
    else:
        nib = np.empty((g, 128, n, 4), np.uint8)
        nib[..., 0::2] = words & 0xF
        nib[..., 1::2] = words >> 4
        vals = E2M1[nib]
    vals = vals * np.repeat(np.exp2(scales.astype(np.float64) - 127.0), 8, axis=1)[..., None]
    return vals.transpose(0, 1, 3, 2).reshape(g * 512, n)


def sigmoid(v):
    return 1.0 / (1.0 + np.exp(-v))


D, K, T, I, Q = 512, 512, 1024, 512, 128


def setup_inputs():
    n = np.random.standard_normal
    idx = np.stack([np.random.permutation(T)[:I] for _ in range(8)])
    idx2 = np.stack([np.random.permutation(T)[:I] for _ in range(8)])
    idx3 = np.stack([np.random.permutation(T)[:I] for _ in range(8)])
    idx4 = np.stack([np.random.permutation(T)[:I] for _ in range(8)])
    fd = mx_kscale(D)
    fk = mx_kscale(K)
    wqp = pack_weight(n((D, K)) * 1.0 / np.sqrt(D) * fd[:, None] * fk, "e4m3")
    keysp = pack_weight(n((K, T)) * 1.0 / np.sqrt(K) / fk[:, None], "e2m1")
    tagsp = pack_weight(n((D, T)) * 0.5 / np.sqrt(D) * fd[:, None], "e4m3")
    return {
        "states": (n((D, Q)) * 0.95 / fd[:, None]).astype(np.float32),
        "wq_words": wqp[0],
        "wq_scales": wqp[1],
        "keys_words": keysp[0],
        "keys_scales": keysp[1],
        "tags_words": tagsp[0],
        "tags_scales": tagsp[1],
        "thr": (np.random.uniform(-0.6, 0.6, (Q, 1))).astype(np.float32),
        "slope": (np.random.uniform(1.0, 3.0, (Q, 1))).astype(np.float32),
        "offs": striped8(idx),
        "offs2": striped8(idx2),
        "offs3": striped8(idx3),
        "offs4": striped8(idx4),
    }


def reference(states, wq_words, wq_scales, keys_words, keys_scales, tags_words, tags_scales, thr, slope, offs, offs2, offs3, offs4):
    idx = unstriped8(offs)
    idx2 = unstriped8(offs2)
    idx3 = unstriped8(offs3)
    idx4 = unstriped8(offs4)
    wqu = unpack_weight(wq_words, wq_scales, "e4m3")
    keysu = unpack_weight(keys_words, keys_scales, "e2m1")
    tagsu = unpack_weight(tags_words, tags_scales, "e4m3")
    statesq = mxq(f64(states), 0, "e4m3")
    qv = wqu.T @ statesq
    qvq = mxq(qv, 0, "e4m3")
    a = qvq.T @ keysu + statesq.T @ tagsu
    s1 = sigmoid(pick8(a, idx, 16) * f64(slope) + f64(thr))
    f1 = np.zeros((Q, T))
    f1[np.arange(Q)[:, None], idx2[np.arange(Q) % 128 // 16]] = s1
    f2 = np.zeros((Q, T))
    f2[np.arange(Q)[:, None], idx3[np.arange(Q) % 128 // 16]] = s1
    r = f1 - f2
    cc = a + r * 2.0
    y = np.maximum(pick8(cc, idx4, 16), pick8(cc, idx2, 16))
    return y

@@ -1,0 +1,155 @@
+from contextlib import ExitStack
+
+import concourse.mybir as mybir
+
+D, K, T, SLOTS, Q = 512, 512, 1024, 512, 128
+FLOPS = 2 * D * K * Q + 2 * K * T * Q + 2 * D * T * Q
+
+F32 = mybir.dt.float32
+BF16 = mybir.dt.bfloat16
+I32 = mybir.dt.int32
+U32 = mybir.dt.uint32
+U16 = mybir.dt.uint16
+U8 = mybir.dt.uint8
+FP8X4 = mybir.dt.float8_e4m3fn_x4
+FP4X4 = mybir.dt.float4_e2m1fn_x4
+ALU = mybir.AluOpType
+ACT = mybir.ActivationFunctionType
+
+P = 128
+PACK = 4
+QUADRANT = 32
+TOKEN_TILE = 256
+HALF = SLOTS // 2
+PER_COLUMN = 16
+
+
+def load_scale_rows(engine, tile, scales):
+    for r in range(PACK):
+        engine.dma_start(out=tile[r:P:QUADRANT, :].bitcast(I32), in_=scales[0, r:16:PACK, :].bitcast(I32))
+
+
+def half_of(offsets, h):
+    return offsets[:, h * HALF // PER_COLUMN : (h + 1) * HALF // PER_COLUMN]
+
+
+def tile_attend_lenders_madeparts_kernel(
+    tc, states, wq_words, wq_scales, keys_words, keys_scales, tags_words, tags_scales, thr, slope, offs, offs2, offs3, offs4, out
+):
+    nc = tc.nc
+    with ExitStack() as ctx:
+        sb = ctx.enter_context(tc.tile_pool(name="sb", bufs=1))
+        psum = ctx.enter_context(tc.psum_pool(name="psum", bufs=1))
+
+        wq_scale_raw = sb.tile([P, K], U8, align_bytes=64)
+        tags_scale = sb.tile([P, T], U8, align_bytes=64)
+        keys_scale = sb.tile([P, T], U8, align_bytes=64)
+        f1 = sb.tile([P, T], F32)
+        f2 = sb.tile([P, T], F32)
+        nc.vector.memset(wq_scale_raw[:].bitcast(I32), 0)
+        nc.vector.memset(tags_scale[:].bitcast(I32), 0)
+        nc.vector.memset(keys_scale[:].bitcast(I32), 0)
+        nc.vector.memset(f2[:], 0.0)
+        nc.vector.memset(f1[:], 0.0)
+
+        states_raw = sb.tile([P, PACK, Q], F32)
+        wq_raw = sb.tile([P, K], U32)
+        tags_code = sb.tile([P, T], U32, align_bytes=64)
+        keys_code = sb.tile([P, 2 * T], U8, align_bytes=64)
+        nc.sync.dma_start(out=states_raw[:], in_=states.rearrange("(p j) q -> p j q", j=PACK))
+        load_scale_rows(nc.scalar, wq_scale_raw, wq_scales)
+        nc.sync.dma_start(out=wq_raw[:].bitcast(I32), in_=wq_words[0].rearrange("p n t -> p (n t)").bitcast(I32))
+        nc.sync.dma_start(out=tags_code[:].bitcast(I32), in_=tags_words[0].rearrange("p n t -> p (n t)").bitcast(I32))
+        nc.sync.dma_start(out=keys_code[:].bitcast(I32), in_=keys_words[0].bitcast(I32))
+        load_scale_rows(nc.sync, tags_scale, tags_scales)
+        load_scale_rows(nc.sync, keys_scale, keys_scales)
+        idx_gate = sb.tile([P, SLOTS // PER_COLUMN], U16)
+        idx_lender = sb.tile([P, SLOTS // PER_COLUMN], U16)
+        idx_taker = sb.tile([P, SLOTS // PER_COLUMN], U16)
+        idx_other = sb.tile([P, SLOTS // PER_COLUMN], U16)
+        thr_col = sb.tile([P, 1], F32)
+        slope_col = sb.tile([P, 1], F32)
+        nc.sync.dma_start(idx_gate[:], offs)
+        nc.gpsimd.dma_start(out=thr_col[:], in_=thr)
+        nc.gpsimd.dma_start(out=slope_col[:], in_=slope)
+        nc.sync.dma_start(idx_lender[:], offs3)
+        nc.sync.dma_start(idx_taker[:], offs2)
+        nc.sync.dma_start(idx_other[:], offs4)
+
+        wq_scale = sb.tile([P, PACK, P], U8, align_bytes=64)
+        wq_code = sb.tile([P, PACK, P], U32, align_bytes=64)
+        nc.vector.tensor_copy(out=wq_scale[:].rearrange("p t m -> p m t"), in_=wq_scale_raw[:].rearrange("p (m t) -> p m t", t=PACK))
+        nc.scalar.copy(out=wq_code[:].rearrange("p t m -> p m t"), in_=wq_raw[:].rearrange("p (m t) -> p m t", t=PACK))
+
+        states_bf = sb.tile([P, Q, PACK], BF16, align_bytes=64)
+        states_code = sb.tile([P, Q], U32, align_bytes=64)
+        states_scale = sb.tile([P, Q], U8, align_bytes=64)
+        nc.vector.tensor_copy(out=states_bf[:], in_=states_raw[:].rearrange("p j q -> p q j"))
+        nc.vector.quantize_mx(out=states_code[:].bitcast(FP8X4), scales=states_scale[:], in_=states_bf[:].rearrange("p q j -> p (q j)"))
+
+        qv_acc = psum.tile([P, PACK, Q], F32)
+        for t in range(PACK):
+            nc.tensor.matmul_mx(
+                out=qv_acc[:, t, :],
+                lhsT=wq_code[:, t, :].bitcast(FP8X4),
+                lhsT_scale=wq_scale[:, t, :],
+                rhs=states_code[:].bitcast(FP8X4),
+                rhs_scale=states_scale[:],
+                start=True,
+                stop=True,
+            )
+        token_tiles = [slice(c, c + TOKEN_TILE) for c in range(0, T, TOKEN_TILE)]
+        a_acc = [psum.tile([P, TOKEN_TILE], F32, name=f"a_acc{j}") for j in range(len(token_tiles))]
+        for acc, cols in zip(a_acc, token_tiles):
+            nc.tensor.matmul_mx(
+                out=acc[:],
+                lhsT=states_code[:].bitcast(FP8X4),
+                lhsT_scale=states_scale[:],
+                rhs=tags_code[:, cols].bitcast(FP8X4),
+                rhs_scale=tags_scale[:, cols],
+                start=True,
+                stop=False,
+            )
+
+        qv_bf = sb.tile([P, Q, PACK], BF16, align_bytes=64)
+        qv_code = sb.tile([P, Q], U32, align_bytes=64)
+        qv_scale = sb.tile([P, Q], U8, align_bytes=64)
+        nc.scalar.copy(out=qv_bf[:], in_=qv_acc[:].rearrange("p t q -> p q t"))
+        nc.vector.quantize_mx(out=qv_code[:].bitcast(FP8X4), scales=qv_scale[:], in_=qv_bf[:].rearrange("p q t -> p (q t)"))
+
+        a = sb.tile([P, T], F32)
+        for acc, cols in zip(a_acc, token_tiles):
+            nc.tensor.matmul_mx(
+                out=acc[:],
+                lhsT=qv_code[:].bitcast(FP8X4),
+                lhsT_scale=qv_scale[:],
+                rhs=keys_code[:, 2 * cols.start : 2 * cols.stop].bitcast(FP4X4),
+                rhs_scale=keys_scale[:, cols],
+                start=False,
+                stop=True,
+            )
+            nc.vector.tensor_copy(out=a[:, cols], in_=acc[:])
+
+        halves = [slice(h * HALF, (h + 1) * HALF) for h in range(2)]
+        s1 = sb.tile([P, SLOTS], F32)
+        for h, cols in enumerate(halves):
+            nc.scalar.activation(
+                out=s1[:, cols], in_=a[:].indirect(half_of(idx_gate, h)), func=ACT.Sigmoid, bias=thr_col[:], scale=slope_col[:]
+            )
+        for h, cols in enumerate(halves):
+            nc.vector.tensor_copy(out=f2[:].indirect(half_of(idx_lender, h)), in_=s1[:, cols])
+        nc.vector.tensor_copy(out=f1[:].indirect(idx_taker[:]), in_=s1[:])
+
+        r = sb.tile([P, T], F32)
+        cc = sb.tile([P, T], F32)
+        nc.vector.tensor_tensor(out=r[:], in0=f1[:], in1=f2[:], op=ALU.subtract)
+        nc.vector.scalar_tensor_tensor(out=cc[:], in0=r[:], scalar=2.0, in1=a[:], op0=ALU.mult, op1=ALU.add)
+
+        at_other = sb.tile([P, SLOTS], F32)
+        at_taker = sb.tile([P, SLOTS], F32)
+        y = sb.tile([P, SLOTS], F32)
+        for h, cols in enumerate(halves):
+            nc.scalar.activation(out=at_taker[:, cols], in_=cc[:].indirect(half_of(idx_taker, h)), func=ACT.Copy)
+            nc.vector.tensor_copy(out=at_other[:, cols], in_=cc[:].indirect(half_of(idx_other, h)))
+            nc.vector.tensor_tensor(out=y[:, cols], in0=at_other[:, cols], in1=at_taker[:, cols], op=ALU.max)
+            nc.sync.dma_start(out=out[:, cols], in_=y[:, cols])

@@ -1,6 +1,7 @@
 from contextlib import ExitStack
 
 import concourse.mybir as mybir
+from concourse.masks import make_identity
 
 D, K, T, SLOTS, Q = 512, 512, 1024, 512, 128
 FLOPS = 2 * D * K * Q + 2 * K * T * Q + 2 * D * T * Q
@@ -22,10 +23,11 @@ QUADRANT = 32
 TOKEN_TILE = 256
 HALF = SLOTS // 2
 PER_COLUMN = 16
+BANK = 512
 
 
-def load_scale_rows(engine, tile, scales):
-    for r in range(PACK):
+def load_scale_rows(engine, tile, scales, rows=range(PACK)):
+    for r in rows:
         engine.dma_start(out=tile[r:P:QUADRANT, :].bitcast(I32), in_=scales[0, r:16:PACK, :].bitcast(I32))
 
 
@@ -49,19 +51,22 @@ def tile_attend_lenders_madeparts_kernel(
         nc.vector.memset(wq_scale_raw[:].bitcast(I32), 0)
         nc.vector.memset(tags_scale[:].bitcast(I32), 0)
         nc.vector.memset(keys_scale[:].bitcast(I32), 0)
-        nc.vector.memset(f2[:], 0.0)
         nc.vector.memset(f1[:], 0.0)
+        nc.vector.memset(f2[:], 0.0)
+        identity = sb.tile([P, P], F32)
+        make_identity(nc, identity[:])
 
         states_raw = sb.tile([P, PACK, Q], F32)
         wq_raw = sb.tile([P, K], U32)
         tags_code = sb.tile([P, T], U32, align_bytes=64)
         keys_code = sb.tile([P, 2 * T], U8, align_bytes=64)
         nc.sync.dma_start(out=states_raw[:], in_=states.rearrange("(p j) q -> p j q", j=PACK))
-        load_scale_rows(nc.scalar, wq_scale_raw, wq_scales)
+        load_scale_rows(nc.sync, wq_scale_raw, wq_scales)
         nc.sync.dma_start(out=wq_raw[:].bitcast(I32), in_=wq_words[0].rearrange("p n t -> p (n t)").bitcast(I32))
-        nc.sync.dma_start(out=tags_code[:].bitcast(I32), in_=tags_words[0].rearrange("p n t -> p (n t)").bitcast(I32))
         nc.sync.dma_start(out=keys_code[:].bitcast(I32), in_=keys_words[0].bitcast(I32))
-        load_scale_rows(nc.sync, tags_scale, tags_scales)
+        load_scale_rows(nc.sync, tags_scale, tags_scales, range(1))
+        nc.sync.dma_start(out=tags_code[:].bitcast(I32), in_=tags_words[0].rearrange("p n t -> p (n t)").bitcast(I32))
+        load_scale_rows(nc.sync, tags_scale, tags_scales, range(1, PACK))
         load_scale_rows(nc.sync, keys_scale, keys_scales)
         idx_gate = sb.tile([P, SLOTS // PER_COLUMN], U16)
         idx_lender = sb.tile([P, SLOTS // PER_COLUMN], U16)
@@ -70,21 +75,21 @@ def tile_attend_lenders_madeparts_kernel(
         thr_col = sb.tile([P, 1], F32)
         slope_col = sb.tile([P, 1], F32)
         nc.sync.dma_start(idx_gate[:], offs)
-        nc.gpsimd.dma_start(out=thr_col[:], in_=thr)
-        nc.gpsimd.dma_start(out=slope_col[:], in_=slope)
-        nc.sync.dma_start(idx_lender[:], offs3)
+        nc.sync.dma_start(out=thr_col[:], in_=thr)
+        nc.sync.dma_start(out=slope_col[:], in_=slope)
         nc.sync.dma_start(idx_taker[:], offs2)
+        nc.sync.dma_start(idx_lender[:], offs3)
         nc.sync.dma_start(idx_other[:], offs4)
 
         wq_scale = sb.tile([P, PACK, P], U8, align_bytes=64)
         wq_code = sb.tile([P, PACK, P], U32, align_bytes=64)
-        nc.vector.tensor_copy(out=wq_scale[:].rearrange("p t m -> p m t"), in_=wq_scale_raw[:].rearrange("p (m t) -> p m t", t=PACK))
         nc.scalar.copy(out=wq_code[:].rearrange("p t m -> p m t"), in_=wq_raw[:].rearrange("p (m t) -> p m t", t=PACK))
 
         states_bf = sb.tile([P, Q, PACK], BF16, align_bytes=64)
         states_code = sb.tile([P, Q], U32, align_bytes=64)
         states_scale = sb.tile([P, Q], U8, align_bytes=64)
         nc.vector.tensor_copy(out=states_bf[:], in_=states_raw[:].rearrange("p j q -> p q j"))
+        nc.vector.tensor_copy(out=wq_scale[:].rearrange("p t m -> p m t"), in_=wq_scale_raw[:].rearrange("p (m t) -> p m t", t=PACK))
         nc.vector.quantize_mx(out=states_code[:].bitcast(FP8X4), scales=states_scale[:], in_=states_bf[:].rearrange("p q j -> p (q j)"))
 
         qv_acc = psum.tile([P, PACK, Q], F32)
@@ -137,13 +142,34 @@ def tile_attend_lenders_madeparts_kernel(
                 out=s1[:, cols], in_=a[:].indirect(half_of(idx_gate, h)), func=ACT.Sigmoid, bias=thr_col[:], scale=slope_col[:]
             )
         for h, cols in enumerate(halves):
-            nc.vector.tensor_copy(out=f2[:].indirect(half_of(idx_lender, h)), in_=s1[:, cols])
-        nc.vector.tensor_copy(out=f1[:].indirect(idx_taker[:]), in_=s1[:])
+            nc.vector.tensor_tensor(out=f1[:].indirect(half_of(idx_taker, h)), in0=s1[:, cols], in1=s1[:, cols], op=ALU.add)
+        s1_twice = sb.tile([P, SLOTS], F32)
+        nc.scalar.activation(out=s1_twice[:], in_=s1[:], func=ACT.Copy, scale=2.0)
+        nc.vector.tensor_copy(out=f2[:].indirect(idx_lender[:]), in_=s1_twice[:])
 
-        r = sb.tile([P, T], F32)
+        blocks = TOKEN_TILE // P
+        turned_acc = [psum.tile([P, TOKEN_TILE], F32, name=f"turned_acc{j}", tag=f"a_acc{j}") for j in range(len(token_tiles))]
+        for acc, cols in zip(turned_acc, token_tiles):
+            for b in range(blocks):
+                nc.tensor.matmul(
+                    acc[:, b * P : (b + 1) * P], a[:, cols.start + b * P : cols.start + (b + 1) * P], identity[:],
+                    start=(b == 0), stop=False, is_transpose=True,
+                )
+        turned = sb.tile([P, T], F32)
+        for acc, cols in zip(turned_acc, token_tiles):
+            for b in range(blocks):
+                nc.tensor.matmul(
+                    acc[:, b * P : (b + 1) * P], f1[:, cols.start + b * P : cols.start + (b + 1) * P], identity[:],
+                    start=False, stop=(b == blocks - 1), is_transpose=True,
+                )
+            nc.scalar.copy(out=turned[:, cols], in_=acc[:])
         cc = sb.tile([P, T], F32)
-        nc.vector.tensor_tensor(out=r[:], in0=f1[:], in1=f2[:], op=ALU.subtract)
-        nc.vector.scalar_tensor_tensor(out=cc[:], in0=r[:], scalar=2.0, in1=a[:], op0=ALU.mult, op1=ALU.add)
+        for u in range(T // BANK):
+            back = psum.tile([P, BANK], F32, name=f"back{u}")
+            for c in range(0, BANK, P):
+                nc.tensor.transpose(back[:, c : c + P], turned[:, u * BANK + c : u * BANK + c + P], identity[:])
+            cols = slice(u * BANK, (u + 1) * BANK)
+            nc.vector.tensor_tensor(out=cc[:, cols], in0=back[:], in1=f2[:, cols], op=ALU.subtract)
 
         at_other = sb.tile([P, SLOTS], F32)
         at_taker = sb.tile([P, SLOTS], F32)

@@ -56,6 +56,11 @@ def tile_attend_lenders_madeparts_kernel(
         identity = sb.tile([P, P], F32)
         make_identity(nc, identity[:])
 
+        warm_in = sb.tile([P, 1], F32)
+        warm_out = sb.tile([P, 1], F32)
+        nc.gpsimd.memset(warm_in[:], 0.0)
+        nc.scalar.activation(out=warm_out[:], in_=warm_in[:], func=ACT.Sigmoid)
+
         states_raw = sb.tile([P, PACK, Q], F32)
         wq_raw = sb.tile([P, K], U32)
         tags_code = sb.tile([P, T], U32, align_bytes=64)

@@ -20,19 +20,25 @@ ACT = mybir.ActivationFunctionType
 P = 128
 PACK = 4
 QUADRANT = 32
-TOKEN_TILE = 256
+SCALE_ROWS = 16
+ENTRIES_PER_COLUMN = 16
 HALF = SLOTS // 2
-PER_COLUMN = 16
-BANK = 512
+SCORE_EDGES = (0, 256, 512, 768, 896, T)
+TURN = 256
+SUM_EDGES = (0, 256, 768, T)
 
 
-def load_scale_rows(engine, tile, scales, rows=range(PACK)):
+def spans(edges):
+    return [slice(lo, hi) for lo, hi in zip(edges, edges[1:])]
+
+
+def load_scale_rows(nc, tile, scales, rows):
     for r in rows:
-        engine.dma_start(out=tile[r:P:QUADRANT, :].bitcast(I32), in_=scales[0, r:16:PACK, :].bitcast(I32))
+        nc.sync.dma_start(out=tile[r:P:QUADRANT, :].bitcast(I32), in_=scales[0, r:SCALE_ROWS:PACK, :].bitcast(I32))
 
 
 def half_of(offsets, h):
-    return offsets[:, h * HALF // PER_COLUMN : (h + 1) * HALF // PER_COLUMN]
+    return offsets[:, h * HALF // ENTRIES_PER_COLUMN : (h + 1) * HALF // ENTRIES_PER_COLUMN]
 
 
 def tile_attend_lenders_madeparts_kernel(
@@ -66,51 +72,60 @@ def tile_attend_lenders_madeparts_kernel(
         tags_code = sb.tile([P, T], U32, align_bytes=64)
         keys_code = sb.tile([P, 2 * T], U8, align_bytes=64)
         nc.sync.dma_start(out=states_raw[:], in_=states.rearrange("(p j) q -> p j q", j=PACK))
-        load_scale_rows(nc.sync, wq_scale_raw, wq_scales)
+        load_scale_rows(nc, wq_scale_raw, wq_scales, range(PACK))
         nc.sync.dma_start(out=wq_raw[:].bitcast(I32), in_=wq_words[0].rearrange("p n t -> p (n t)").bitcast(I32))
         nc.sync.dma_start(out=keys_code[:].bitcast(I32), in_=keys_words[0].bitcast(I32))
-        load_scale_rows(nc.sync, tags_scale, tags_scales, range(1))
+        load_scale_rows(nc, tags_scale, tags_scales, range(1))
         nc.sync.dma_start(out=tags_code[:].bitcast(I32), in_=tags_words[0].rearrange("p n t -> p (n t)").bitcast(I32))
-        load_scale_rows(nc.sync, tags_scale, tags_scales, range(1, PACK))
-        load_scale_rows(nc.sync, keys_scale, keys_scales)
-        idx_gate = sb.tile([P, SLOTS // PER_COLUMN], U16)
-        idx_lender = sb.tile([P, SLOTS // PER_COLUMN], U16)
-        idx_taker = sb.tile([P, SLOTS // PER_COLUMN], U16)
-        idx_other = sb.tile([P, SLOTS // PER_COLUMN], U16)
+        load_scale_rows(nc, tags_scale, tags_scales, range(1, PACK))
+        load_scale_rows(nc, keys_scale, keys_scales, range(PACK))
+        idx = sb.tile([P, SLOTS // ENTRIES_PER_COLUMN], U16)
+        idx3 = sb.tile([P, SLOTS // ENTRIES_PER_COLUMN], U16)
+        idx2 = sb.tile([P, SLOTS // ENTRIES_PER_COLUMN], U16)
+        idx4 = sb.tile([P, SLOTS // ENTRIES_PER_COLUMN], U16)
         thr_col = sb.tile([P, 1], F32)
         slope_col = sb.tile([P, 1], F32)
-        nc.sync.dma_start(idx_gate[:], offs)
+        nc.sync.dma_start(idx[:], offs)
         nc.sync.dma_start(out=thr_col[:], in_=thr)
         nc.sync.dma_start(out=slope_col[:], in_=slope)
-        nc.sync.dma_start(idx_taker[:], offs2)
-        nc.sync.dma_start(idx_lender[:], offs3)
-        nc.sync.dma_start(idx_other[:], offs4)
+        nc.sync.dma_start(idx2[:], offs2)
+        nc.sync.dma_start(idx3[:], offs3)
+        nc.sync.dma_start(idx4[:], offs4)
 
-        wq_scale = sb.tile([P, PACK, P], U8, align_bytes=64)
-        wq_code = sb.tile([P, PACK, P], U32, align_bytes=64)
-        nc.scalar.copy(out=wq_code[:].rearrange("p t m -> p m t"), in_=wq_raw[:].rearrange("p (m t) -> p m t", t=PACK))
+        wq_scale = [sb.tile([P, 2, P], U8, align_bytes=64, name=f"wq_scale{u}") for u in range(2)]
+        wq_code = [sb.tile([P, 2, P], U32, align_bytes=64, name=f"wq_code{u}") for u in range(2)]
+        for u in range(2):
+            nc.scalar.copy(
+                out=wq_code[u][:].rearrange("p t m -> p m t"),
+                in_=wq_raw[:].rearrange("p (m t) -> p m t", t=PACK)[:, :, 2 * u : 2 * u + 2],
+            )
 
         states_bf = sb.tile([P, Q, PACK], BF16, align_bytes=64)
         states_code = sb.tile([P, Q], U32, align_bytes=64)
         states_scale = sb.tile([P, Q], U8, align_bytes=64)
         nc.vector.tensor_copy(out=states_bf[:], in_=states_raw[:].rearrange("p j q -> p q j"))
-        nc.vector.tensor_copy(out=wq_scale[:].rearrange("p t m -> p m t"), in_=wq_scale_raw[:].rearrange("p (m t) -> p m t", t=PACK))
         nc.vector.quantize_mx(out=states_code[:].bitcast(FP8X4), scales=states_scale[:], in_=states_bf[:].rearrange("p q j -> p (q j)"))
+        for u in range(2):
+            nc.vector.tensor_copy(
+                out=wq_scale[u][:].rearrange("p t m -> p m t"),
+                in_=wq_scale_raw[:].rearrange("p (m t) -> p m t", t=PACK)[:, :, 2 * u : 2 * u + 2],
+            )
 
         qv_acc = psum.tile([P, PACK, Q], F32)
         for t in range(PACK):
             nc.tensor.matmul_mx(
                 out=qv_acc[:, t, :],
-                lhsT=wq_code[:, t, :].bitcast(FP8X4),
-                lhsT_scale=wq_scale[:, t, :],
+                lhsT=wq_code[t // 2][:, t % 2, :].bitcast(FP8X4),
+                lhsT_scale=wq_scale[t // 2][:, t % 2, :],
                 rhs=states_code[:].bitcast(FP8X4),
                 rhs_scale=states_scale[:],
                 start=True,
                 stop=True,
             )
-        token_tiles = [slice(c, c + TOKEN_TILE) for c in range(0, T, TOKEN_TILE)]
-        a_acc = [psum.tile([P, TOKEN_TILE], F32, name=f"a_acc{j}") for j in range(len(token_tiles))]
-        for acc, cols in zip(a_acc, token_tiles):
+
+        score_cols = spans(SCORE_EDGES)
+        a_acc = [psum.tile([P, cols.stop - cols.start], F32, name=f"a_acc{j}") for j, cols in enumerate(score_cols)]
+        for acc, cols in zip(a_acc, score_cols):
             nc.tensor.matmul_mx(
                 out=acc[:],
                 lhsT=states_code[:].bitcast(FP8X4),
@@ -128,7 +143,7 @@ def tile_attend_lenders_madeparts_kernel(
         nc.vector.quantize_mx(out=qv_code[:].bitcast(FP8X4), scales=qv_scale[:], in_=qv_bf[:].rearrange("p q t -> p (q t)"))
 
         a = sb.tile([P, T], F32)
-        for acc, cols in zip(a_acc, token_tiles):
+        for j, (acc, cols) in enumerate(zip(a_acc, score_cols)):
             nc.tensor.matmul_mx(
                 out=acc[:],
                 lhsT=qv_code[:].bitcast(FP8X4),
@@ -138,49 +153,63 @@ def tile_attend_lenders_madeparts_kernel(
                 start=False,
                 stop=True,
             )
-            nc.vector.tensor_copy(out=a[:, cols], in_=acc[:])
+            if j % 2 == 1:
+                nc.vector.tensor_copy(out=a[:, cols], in_=acc[:])
+            else:
+                nc.scalar.copy(out=a[:, cols], in_=acc[:])
 
         halves = [slice(h * HALF, (h + 1) * HALF) for h in range(2)]
         s1 = sb.tile([P, SLOTS], F32)
         for h, cols in enumerate(halves):
             nc.scalar.activation(
-                out=s1[:, cols], in_=a[:].indirect(half_of(idx_gate, h)), func=ACT.Sigmoid, bias=thr_col[:], scale=slope_col[:]
+                out=s1[:, cols], in_=a[:].indirect(half_of(idx, h)), func=ACT.Sigmoid, bias=thr_col[:], scale=slope_col[:]
             )
         for h, cols in enumerate(halves):
-            nc.vector.tensor_tensor(out=f1[:].indirect(half_of(idx_taker, h)), in0=s1[:, cols], in1=s1[:, cols], op=ALU.add)
-        s1_twice = sb.tile([P, SLOTS], F32)
-        nc.scalar.activation(out=s1_twice[:], in_=s1[:], func=ACT.Copy, scale=2.0)
-        nc.vector.tensor_copy(out=f2[:].indirect(idx_lender[:]), in_=s1_twice[:])
+            nc.vector.tensor_copy(out=f1[:].indirect(half_of(idx2, h)), in_=s1[:, cols])
 
-        blocks = TOKEN_TILE // P
-        turned_acc = [psum.tile([P, TOKEN_TILE], F32, name=f"turned_acc{j}", tag=f"a_acc{j}") for j in range(len(token_tiles))]
-        for acc, cols in zip(turned_acc, token_tiles):
-            for b in range(blocks):
+        a_half = sb.tile([P, T], F32, tag="thr_col")
+        for cols in score_cols:
+            nc.scalar.activation(out=a_half[:, cols], in_=a[:, cols], func=ACT.Copy, scale=0.5)
+        s1_lent = sb.tile([P, SLOTS], F32)
+        nc.scalar.activation(out=s1_lent[:], in_=s1[:], func=ACT.Copy, scale=-2.0)
+        nc.vector.tensor_copy(out=f2[:].indirect(idx3[:]), in_=s1_lent[:])
+
+        turn_cols = spans(range(0, T + 1, TURN))
+        turned_acc = [psum.tile([P, TURN], F32, name=f"turned_acc{j}", tag=f"a_acc{j}") for j in range(len(turn_cols))]
+        for acc, cols in zip(turned_acc, turn_cols):
+            for c in range(0, TURN, P):
                 nc.tensor.matmul(
-                    acc[:, b * P : (b + 1) * P], a[:, cols.start + b * P : cols.start + (b + 1) * P], identity[:],
-                    start=(b == 0), stop=False, is_transpose=True,
+                    acc[:, c : c + P], a_half[:, cols.start + c : cols.start + c + P], identity[:],
+                    start=(c == 0), stop=False, is_transpose=True,
                 )
         turned = sb.tile([P, T], F32)
-        for acc, cols in zip(turned_acc, token_tiles):
-            for b in range(blocks):
+        for acc, cols in zip(turned_acc, turn_cols):
+            for c in range(0, TURN, P):
                 nc.tensor.matmul(
-                    acc[:, b * P : (b + 1) * P], f1[:, cols.start + b * P : cols.start + (b + 1) * P], identity[:],
-                    start=False, stop=(b == blocks - 1), is_transpose=True,
+                    acc[:, c : c + P], f1[:, cols.start + c : cols.start + c + P], identity[:],
+                    start=False, stop=(c == TURN - P), is_transpose=True,
                 )
-            nc.scalar.copy(out=turned[:, cols], in_=acc[:])
-        cc = sb.tile([P, T], F32)
-        for u in range(T // BANK):
-            back = psum.tile([P, BANK], F32, name=f"back{u}")
-            for c in range(0, BANK, P):
-                nc.tensor.transpose(back[:, c : c + P], turned[:, u * BANK + c : u * BANK + c + P], identity[:])
-            cols = slice(u * BANK, (u + 1) * BANK)
-            nc.vector.tensor_tensor(out=cc[:, cols], in0=back[:], in1=f2[:, cols], op=ALU.subtract)
+            nc.scalar.activation(out=turned[:, cols], in_=acc[:], func=ACT.Copy, scale=2.0)
 
-        at_other = sb.tile([P, SLOTS], F32)
-        at_taker = sb.tile([P, SLOTS], F32)
+        cc = sb.tile([P, T], F32)
+        for j, cols in enumerate(spans(SUM_EDGES)):
+            width = cols.stop - cols.start
+            back = psum.tile([P, width], F32, name=f"back{j}", tag="qv_acc" if j == 0 else f"back{j}")
+            for c in range(0, width, P):
+                nc.tensor.transpose(back[:, c : c + P], turned[:, cols.start + c : cols.start + c + P], identity[:])
+            if j == 0:
+                back_sb = sb.tile([P, width], F32)
+                nc.scalar.copy(out=back_sb[:], in_=back[:])
+                nc.gpsimd.tensor_tensor(out=cc[:, cols], in0=f2[:, cols], in1=back_sb[:], op=ALU.add)
+            else:
+                nc.vector.tensor_tensor(out=cc[:, cols], in0=f2[:, cols], in1=back[:], op=ALU.add)
+
+        at_idx4 = sb.tile([P, SLOTS], F32)
+        at_idx2 = sb.tile([P, SLOTS], F32)
         y = sb.tile([P, SLOTS], F32)
         for h, cols in enumerate(halves):
-            nc.scalar.activation(out=at_taker[:, cols], in_=cc[:].indirect(half_of(idx_taker, h)), func=ACT.Copy)
-            nc.vector.tensor_copy(out=at_other[:, cols], in_=cc[:].indirect(half_of(idx_other, h)))
-            nc.vector.tensor_tensor(out=y[:, cols], in0=at_other[:, cols], in1=at_taker[:, cols], op=ALU.max)
+            nc.scalar.activation(out=at_idx2[:, cols], in_=cc[:].indirect(half_of(idx2, h)), func=ACT.Copy)
+            nc.vector.tensor_copy(out=at_idx4[:, cols], in_=cc[:].indirect(half_of(idx4, h)))
+        for cols in halves:
+            nc.vector.tensor_tensor(out=y[:, cols], in0=at_idx4[:, cols], in1=at_idx2[:, cols], op=ALU.max)
             nc.sync.dma_start(out=out[:, cols], in_=y[:, cols])

from contextlib import ExitStack

import concourse.mybir as mybir
from concourse.masks import make_identity

D, K, T, SLOTS, Q = 512, 512, 1024, 512, 128
FLOPS = 2 * D * K * Q + 2 * K * T * Q + 2 * D * T * Q

F32 = mybir.dt.float32
BF16 = mybir.dt.bfloat16
I32 = mybir.dt.int32
U32 = mybir.dt.uint32
U16 = mybir.dt.uint16
U8 = mybir.dt.uint8
FP8X4 = mybir.dt.float8_e4m3fn_x4
FP4X4 = mybir.dt.float4_e2m1fn_x4
ALU = mybir.AluOpType
ACT = mybir.ActivationFunctionType

P = 128
PACK = 4
QUADRANT = 32
SCALE_ROWS = 16
ENTRIES_PER_COLUMN = 16
HALF = SLOTS // 2
SCORE_EDGES = (0, 256, 512, 768, 896, T)
TURN = 256
SUM_EDGES = (0, 256, 768, T)


def spans(edges):
    return [slice(lo, hi) for lo, hi in zip(edges, edges[1:])]


def load_scale_rows(nc, tile, scales, rows):
    for r in rows:
        nc.sync.dma_start(out=tile[r:P:QUADRANT, :].bitcast(I32), in_=scales[0, r:SCALE_ROWS:PACK, :].bitcast(I32))


def half_of(offsets, h):
    return offsets[:, h * HALF // ENTRIES_PER_COLUMN : (h + 1) * HALF // ENTRIES_PER_COLUMN]


def tile_attend_lenders_madeparts_kernel(
    tc, states, wq_words, wq_scales, keys_words, keys_scales, tags_words, tags_scales, thr, slope, offs, offs2, offs3, offs4, out
):
    nc = tc.nc
    with ExitStack() as ctx:
        sb = ctx.enter_context(tc.tile_pool(name="sb", bufs=1))
        psum = ctx.enter_context(tc.psum_pool(name="psum", bufs=1))

        wq_scale_raw = sb.tile([P, K], U8, align_bytes=64)
        tags_scale = sb.tile([P, T], U8, align_bytes=64)
        keys_scale = sb.tile([P, T], U8, align_bytes=64)
        f1 = sb.tile([P, T], F32)
        f2 = sb.tile([P, T], F32)
        nc.vector.memset(wq_scale_raw[:].bitcast(I32), 0)
        nc.vector.memset(tags_scale[:].bitcast(I32), 0)
        nc.vector.memset(keys_scale[:].bitcast(I32), 0)
        nc.vector.memset(f1[:], 0.0)
        nc.vector.memset(f2[:], 0.0)
        identity = sb.tile([P, P], F32)
        make_identity(nc, identity[:])

        warm_in = sb.tile([P, 1], F32)
        warm_out = sb.tile([P, 1], F32)
        nc.gpsimd.memset(warm_in[:], 0.0)
        nc.scalar.activation(out=warm_out[:], in_=warm_in[:], func=ACT.Sigmoid)

        states_raw = sb.tile([P, PACK, Q], F32)
        wq_raw = sb.tile([P, K], U32)
        tags_code = sb.tile([P, T], U32, align_bytes=64)
        keys_code = sb.tile([P, 2 * T], U8, align_bytes=64)
        nc.sync.dma_start(out=states_raw[:], in_=states.rearrange("(p j) q -> p j q", j=PACK))
        load_scale_rows(nc, wq_scale_raw, wq_scales, range(PACK))
        nc.sync.dma_start(out=wq_raw[:].bitcast(I32), in_=wq_words[0].rearrange("p n t -> p (n t)").bitcast(I32))
        nc.sync.dma_start(out=keys_code[:].bitcast(I32), in_=keys_words[0].bitcast(I32))
        load_scale_rows(nc, tags_scale, tags_scales, range(1))
        nc.sync.dma_start(out=tags_code[:].bitcast(I32), in_=tags_words[0].rearrange("p n t -> p (n t)").bitcast(I32))
        load_scale_rows(nc, tags_scale, tags_scales, range(1, PACK))
        load_scale_rows(nc, keys_scale, keys_scales, range(PACK))
        idx = sb.tile([P, SLOTS // ENTRIES_PER_COLUMN], U16)
        idx3 = sb.tile([P, SLOTS // ENTRIES_PER_COLUMN], U16)
        idx2 = sb.tile([P, SLOTS // ENTRIES_PER_COLUMN], U16)
        idx4 = sb.tile([P, SLOTS // ENTRIES_PER_COLUMN], U16)
        thr_col = sb.tile([P, 1], F32)
        slope_col = sb.tile([P, 1], F32)
        nc.sync.dma_start(idx[:], offs)
        nc.sync.dma_start(out=thr_col[:], in_=thr)
        nc.sync.dma_start(out=slope_col[:], in_=slope)
        nc.sync.dma_start(idx2[:], offs2)
        nc.sync.dma_start(idx3[:], offs3)
        nc.sync.dma_start(idx4[:], offs4)

        wq_scale = [sb.tile([P, 2, P], U8, align_bytes=64, name=f"wq_scale{u}") for u in range(2)]
        wq_code = [sb.tile([P, 2, P], U32, align_bytes=64, name=f"wq_code{u}") for u in range(2)]
        for u in range(2):
            nc.scalar.copy(
                out=wq_code[u][:].rearrange("p t m -> p m t"),
                in_=wq_raw[:].rearrange("p (m t) -> p m t", t=PACK)[:, :, 2 * u : 2 * u + 2],
            )

        states_bf = sb.tile([P, Q, PACK], BF16, align_bytes=64)
        states_code = sb.tile([P, Q], U32, align_bytes=64)
        states_scale = sb.tile([P, Q], U8, align_bytes=64)
        nc.vector.tensor_copy(out=states_bf[:], in_=states_raw[:].rearrange("p j q -> p q j"))
        nc.vector.quantize_mx(out=states_code[:].bitcast(FP8X4), scales=states_scale[:], in_=states_bf[:].rearrange("p q j -> p (q j)"))
        for u in range(2):
            nc.vector.tensor_copy(
                out=wq_scale[u][:].rearrange("p t m -> p m t"),
                in_=wq_scale_raw[:].rearrange("p (m t) -> p m t", t=PACK)[:, :, 2 * u : 2 * u + 2],
            )

        qv_acc = psum.tile([P, PACK, Q], F32)
        for t in range(PACK):
            nc.tensor.matmul_mx(
                out=qv_acc[:, t, :],
                lhsT=wq_code[t // 2][:, t % 2, :].bitcast(FP8X4),
                lhsT_scale=wq_scale[t // 2][:, t % 2, :],
                rhs=states_code[:].bitcast(FP8X4),
                rhs_scale=states_scale[:],
                start=True,
                stop=True,
            )

        score_cols = spans(SCORE_EDGES)
        a_acc = [psum.tile([P, cols.stop - cols.start], F32, name=f"a_acc{j}") for j, cols in enumerate(score_cols)]
        for acc, cols in zip(a_acc, score_cols):
            nc.tensor.matmul_mx(
                out=acc[:],
                lhsT=states_code[:].bitcast(FP8X4),
                lhsT_scale=states_scale[:],
                rhs=tags_code[:, cols].bitcast(FP8X4),
                rhs_scale=tags_scale[:, cols],
                start=True,
                stop=False,
            )

        qv_bf = sb.tile([P, Q, PACK], BF16, align_bytes=64)
        qv_code = sb.tile([P, Q], U32, align_bytes=64)
        qv_scale = sb.tile([P, Q], U8, align_bytes=64)
        nc.scalar.copy(out=qv_bf[:], in_=qv_acc[:].rearrange("p t q -> p q t"))
        nc.vector.quantize_mx(out=qv_code[:].bitcast(FP8X4), scales=qv_scale[:], in_=qv_bf[:].rearrange("p q t -> p (q t)"))

        a = sb.tile([P, T], F32)
        for j, (acc, cols) in enumerate(zip(a_acc, score_cols)):
            nc.tensor.matmul_mx(
                out=acc[:],
                lhsT=qv_code[:].bitcast(FP8X4),
                lhsT_scale=qv_scale[:],
                rhs=keys_code[:, 2 * cols.start : 2 * cols.stop].bitcast(FP4X4),
                rhs_scale=keys_scale[:, cols],
                start=False,
                stop=True,
            )
            if j % 2 == 1:
                nc.vector.tensor_copy(out=a[:, cols], in_=acc[:])
            else:
                nc.scalar.copy(out=a[:, cols], in_=acc[:])

        halves = [slice(h * HALF, (h + 1) * HALF) for h in range(2)]
        s1 = sb.tile([P, SLOTS], F32)
        for h, cols in enumerate(halves):
            nc.scalar.activation(
                out=s1[:, cols], in_=a[:].indirect(half_of(idx, h)), func=ACT.Sigmoid, bias=thr_col[:], scale=slope_col[:]
            )
        for h, cols in enumerate(halves):
            nc.vector.tensor_copy(out=f1[:].indirect(half_of(idx2, h)), in_=s1[:, cols])

        a_half = sb.tile([P, T], F32, tag="thr_col")
        for cols in score_cols:
            nc.scalar.activation(out=a_half[:, cols], in_=a[:, cols], func=ACT.Copy, scale=0.5)
        s1_lent = sb.tile([P, SLOTS], F32)
        nc.scalar.activation(out=s1_lent[:], in_=s1[:], func=ACT.Copy, scale=-2.0)
        nc.vector.tensor_copy(out=f2[:].indirect(idx3[:]), in_=s1_lent[:])

        turn_cols = spans(range(0, T + 1, TURN))
        turned_acc = [psum.tile([P, TURN], F32, name=f"turned_acc{j}", tag=f"a_acc{j}") for j in range(len(turn_cols))]
        for acc, cols in zip(turned_acc, turn_cols):
            for c in range(0, TURN, P):
                nc.tensor.matmul(
                    acc[:, c : c + P], a_half[:, cols.start + c : cols.start + c + P], identity[:],
                    start=(c == 0), stop=False, is_transpose=True,
                )
        turned = sb.tile([P, T], F32)
        for acc, cols in zip(turned_acc, turn_cols):
            for c in range(0, TURN, P):
                nc.tensor.matmul(
                    acc[:, c : c + P], f1[:, cols.start + c : cols.start + c + P], identity[:],
                    start=False, stop=(c == TURN - P), is_transpose=True,
                )
            nc.scalar.activation(out=turned[:, cols], in_=acc[:], func=ACT.Copy, scale=2.0)

        cc = sb.tile([P, T], F32)
        for j, cols in enumerate(spans(SUM_EDGES)):
            width = cols.stop - cols.start
            back = psum.tile([P, width], F32, name=f"back{j}", tag="qv_acc" if j == 0 else f"back{j}")
            for c in range(0, width, P):
                nc.tensor.transpose(back[:, c : c + P], turned[:, cols.start + c : cols.start + c + P], identity[:])
            if j == 0:
                back_sb = sb.tile([P, width], F32)
                nc.scalar.copy(out=back_sb[:], in_=back[:])
                nc.gpsimd.tensor_tensor(out=cc[:, cols], in0=f2[:, cols], in1=back_sb[:], op=ALU.add)
            else:
                nc.vector.tensor_tensor(out=cc[:, cols], in0=f2[:, cols], in1=back[:], op=ALU.add)

        at_idx4 = sb.tile([P, SLOTS], F32)
        at_idx2 = sb.tile([P, SLOTS], F32)
        y = sb.tile([P, SLOTS], F32)
        for h, cols in enumerate(halves):
            nc.scalar.activation(out=at_idx2[:, cols], in_=cc[:].indirect(half_of(idx2, h)), func=ACT.Copy)
            nc.vector.tensor_copy(out=at_idx4[:, cols], in_=cc[:].indirect(half_of(idx4, h)))
        for cols in halves:
            nc.vector.tensor_tensor(out=y[:, cols], in0=at_idx4[:, cols], in1=at_idx2[:, cols], op=ALU.max)
            nc.sync.dma_start(out=out[:, cols], in_=y[:, cols])
